import numpy as np, ml_dtypes
CORES = [1,5,17,21,33,37,49,53]
N = 8
import mx_ref
BF = ml_dtypes.bfloat16
def gentries(a):
    return np.ascontiguousarray(a.reshape(8, 16, -1).transpose(0, 2, 1)).reshape(8, -1)
def gtable(e):
    e = np.asarray(e); return np.ascontiguousarray(e.reshape(8, -1, 16).transpose(0, 2, 1)).reshape(128, -1).astype(np.int32)
def gcols(t, e):
    v = np.concatenate([t.reshape(8, 16, -1, 4), np.zeros((8, 16, 1, 4), BF)], axis=2)
    return np.ascontiguousarray(np.stack([v[g][:, e[g]] for g in range(8)])).reshape(128, -1)
def f(rng, *shape):
    return mx_ref.flush((rng.standard_normal(shape, dtype=np.float32) * np.exp2(rng.integers(-2, 3, shape[:-1] + (1,)))).astype(BF))
def wide(rng, *shape, cols=0):
    v = rng.standard_normal(shape, dtype=np.float32) * np.exp2(rng.integers(-12, 13, shape)).astype(np.float32)
    if cols: v *= np.repeat(np.exp2(rng.integers(-cols, cols + 1, shape[:-2] + (1, shape[-1] // 4))) * (rng.random(shape[:-2] + (1, shape[-1] // 4)) > 0.0625), 4, axis=-1).astype(np.float32)
    return mx_ref.flush(v.astype(BF))
T, O, K = 256, 2, 256
def lists(rng, alike=False, groups=False, ends=False, few=False):
    c = []
    for r in range(N):
        e = rng.integers(0, K, (8, O, 2, 128))
        if groups: e = np.stack([e[0]] * 8)
        if ends: e = rng.permuted(np.resize([0, K - 1], (8, O, 2, 128)), axis=3)
        if few:
            for m in range(2): e[:, :, m] = rng.permutation(np.resize(rng.permutation(K)[:8], 8 * O * 128)).reshape(8, O, 128)
        c.append(gtable(e.reshape(8, -1)))
    if alike: c = [c[0]] * N
    return np.stack(c)
def setup_inputs(rng):
    return {"x": f(rng, N, 128, 4 * T), "book": np.stack([f(rng, 128, 8 * K)] * N), "cw": lists(rng)}
def setup_inputs_alike(rng):
    d = setup_inputs(rng); d["cw"] = lists(rng, alike=True); return d
def setup_inputs_groups(rng):
    d = setup_inputs(rng); d["cw"] = lists(rng, groups=True); return d
def setup_inputs_ends(rng):
    d = setup_inputs(rng); d["cw"] = lists(rng, ends=True); return d
def setup_inputs_few(rng):
    d = setup_inputs(rng); d["cw"] = lists(rng, few=True); return d
def setup_inputs_spread(rng):
    d = setup_inputs(rng); d["x"] = wide(rng, N, 128, 4 * T, cols=8); d["book"] = np.stack([wide(rng, 128, 8 * K, cols=4)] * N); return d
def check_inputs(d):
    b = []
    for r in range(N):
        if d["cw"][r].min() < 0 or d["cw"][r].max() >= K: b.append("cw")
        if d["book"][r].tobytes() != d["book"][0].tobytes(): b.append("book")
    return b
def reference(x, book, cw):
    W = []
    for s in range(N):
        e = gentries(cw[s])
        for o in range(O):
            a, b = [gcols(np.ascontiguousarray(book[s][:, 4 * K * m:4 * K * m + 4 * K]), e[:, (2 * o + m) * 128:(2 * o + m) * 128 + 128]).astype(np.float32) for m in range(2)]
            W.append(mx_ref.quantize((a + b).astype(BF)))
    y = np.zeros((N, 128, N * O * T), np.float32)
    for r in range(N):
        X = mx_ref.quantize(np.ascontiguousarray(x[r]))
        for i in range(N * O): y[r][:, T * i:T * i + T] = mx_ref.matmul(W[i], X)
    return {"y": y}

from concourse.bass import DstId, RemoteDMATransfer
from concourse.mybir import dt, AluOpType, ActivationFunctionType

N, O, T_COLS, K = 8, 2, 256, 256
W = 128
P = O * W
BANKS = 8

SCRATCH = {
    "cwl": ("sbuf", [128, O, 2, W // 16], "int32"),
    "bk0": ("sbuf", [128, 4 * K], "bfloat16"),
    "bk1": ("sbuf", [128, 4 * K], "bfloat16"),
    "xb": ("sbuf", [128, 4 * T_COLS], "bfloat16"),
    "xq": ("sbuf", [128, T_COLS], "float8_e4m3fn_x4"),
    "xz": ("sbuf", [128, T_COLS], "uint8"),
    "yb": ("sbuf", [128, N * O * T_COLS], "float32"),
}
for _k in range(N):
    SCRATCH["w%d" % _k] = ("sbuf", [128, P], "float8_e4m3fn_x4")
    SCRATCH["z%d" % _k] = ("sbuf", [128, P], "uint8")
    SCRATCH["li%d" % _k] = ("sbuf", [128, 8 * P // 16], "uint16")
for _k in range(4):
    SCRATCH["g%d" % _k] = ("sbuf", [128, 4 * P], "bfloat16")
    SCRATCH["h%d" % _k] = ("sbuf", [128, 4 * P], "bfloat16")
for _k in range(BANKS):
    SCRATCH["ps%d" % _k] = ("psum", [128, 512], "float32")

SEMAPHORES = ["s_cw", "s_b0", "s_b1", "s_x", "s_list", "s_xq", "s_sent", "s_out"]
SEMAPHORES += ["s_g%d%d" % (i, t) for i in range(4) for t in range(4)]
SEMAPHORES += ["s_h%d" % i for i in range(4)] + ["s_q%d" % i for i in range(4)]
SEMAPHORES += ["s_al%d" % s for s in range(N)] + ["s_ar%d" % s for s in range(N)]
SEMAPHORES += ["s_mm%d" % i for i in range(N * O)] + ["s_ev%d" % i for i in range(N * O)]

PLAN = {
    "lists": [2, 3], "codes": [1],
    "tensor": ["own", "mate", "l0", "c0", "l1", "m0", "d0", "m1"],
    "scalar": ["g own", "e own 0", "g l0", "g l1", "e mate 0", "e l0 0", "e l0 1", "e c0 0", "e c0 1", "e m0 0", "e d0 0", "e m1 0"],
    "vector": ["a own", "x", "e own 1", "a l0", "a l1", "e mate 1", "e l1 0", "e l1 1", "e m0 1", "e d0 1", "e m1 1"],
    "store": [["own"], ["mate"], ["l0"], ["c0"], ["l1"], ["m0"], ["d0"], ["m1"]],
    "mate_eng": {"own": "rest", "l0": "rest", "l1": "on"},
}


def bits(engines):
    return sum(1 << e for e in engines)


def rank_program(g, core, T, topo):
    r = T.rank_of(core)
    if r is None:
        return
    cores = T.cores
    chips = sorted(set(topo.chip(c) for c in cores))
    here = chips.index(topo.chip(core))
    same, other = {}, {}
    for s, c in enumerate(cores):
        (same if topo.die(c) == topo.die(core) else other)[chips.index(topo.chip(c))] = s
    role = {"own": r, "mate": other[here]}
    made = {"own": 0}
    for k, v in enumerate(PLAN["lists"]):
        role["l%d" % k], role["m%d" % k] = same[here ^ v], other[here ^ v]
        made["l%d" % k] = k + 1
    for k, v in enumerate(PLAN["codes"]):
        role["c%d" % k], role["d%d" % k] = same[here ^ v], other[here ^ v]
    far = cores[same[here ^ 1]]
    sets = {"on": topo.engines(core, cores[role["mate"]]), "off": topo.engines(core, far)}
    sets["rest"] = [e for e in sets["on"] if e not in sets["off"]]
    off = sets["off"]
    sent = [0]

    def transfer(dst, engines, sem, src, to):
        rid, pid = topo.addr(cores[dst])[:2]
        sent[0] += len(engines)
        return RemoteDMATransfer(dst_ids=[DstId(rid=rid, pnc=pid)], dma_engine_mask=bits(engines),
                                 remote_sem=T.sem[sem], src=src, dst=to)

    def send(s, ways):
        q, z = T["w%d" % s], T["z%d" % s]
        g.remote_dma_fused([transfer(d, e, "s_ar%d" % s, q[:, 0:P].bitcast(dt.uint8), q[:, 0:P].bitcast(dt.uint8))
                            for d, e in ways], local_sem=T.sem.s_sent)
        g.remote_dma_fused([transfer(d, e, "s_ar%d" % s, z[:, 0:P], z[:, 0:P]) for d, e in ways], local_sem=T.sem.s_sent)

    ways, half = [], len(off) // 2
    for k in range(len(PLAN["codes"])):
        ways += [[(role["c%d" % k], off[:half]), (role["d%d" % k], off[half:])]]
    arrive = {"mate": len(sets[PLAN["mate_eng"]["own"]])}
    for k in range(len(PLAN["lists"])):
        arrive["m%d" % k] = len(sets[PLAN["mate_eng"]["l%d" % k]])
    for k in range(len(PLAN["codes"])):
        arrive["c%d" % k] = arrive["d%d" % k] = half

    g.sync.dma_start(T.cwl[:, :, :, :], T.cw[:, :]).then_inc(T.sem.s_cw, 16)
    g.sync.dma_start(T.bk1[:, :], T.book[:, 4 * K:8 * K]).then_inc(T.sem.s_b1, 16)
    g.sync.dma_start(T.bk0[:, :], T.book[:, 0:4 * K]).then_inc(T.sem.s_b0, 16)
    g.sync.dma_start(T.xb[:, :], T.x[:, :]).then_inc(T.sem.s_x, 16)

    n = P // 16
    g.vector.wait_ge(T.sem.s_cw, 16)
    own = T["li%d" % r]
    for m in (1, 0):
        for t in range(4):
            k = (m * 4 + t) * n
            g.vector.tensor_scalar(own[:, k:k + n], T.cwl[:, :, m, :], 4.0, float(t), AluOpType.mult,
                                   AluOpType.add).then_inc(T.sem.s_list, 1)

    nl = len(PLAN["lists"])
    g.wait_ge(T.sem.s_list, 8)
    for k in range(nl):
        g.remote_dma_fused([transfer(role["l%d" % k], off, "s_al%d" % r, own[:, :], own[:, :])], local_sem=T.sem.s_sent)
    g.wait_ge(T.sem.s_q0, 1)
    first = [(role["mate"], sets[PLAN["mate_eng"]["own"]])]
    if PLAN["mate_eng"]["own"] == "rest":
        send(r, first + (ways[0] if ways else []))
        rem = ways[1:]
    else:
        send(r, first)
        rem = ways
    for w in rem:
        send(r, w)
    for k in range(nl):
        g.wait_ge(T.sem["s_q%d" % (k + 1)], 1)
        send(role["l%d" % k], [(role["mate"], sets[PLAN["mate_eng"]["l%d" % k]])])
    g.wait_ge(T.sem.s_sent, sent[0])

    seen = {"scalar": set(), "vector": set()}

    def once(name, q, sem, val):
        if sem not in seen[name]:
            seen[name].add(sem)
            q.wait_ge(T.sem[sem], val)

    def list_wait(name, q, who):
        if who == "own":
            once(name, q, "s_list", 8)
        else:
            once(name, q, "s_al%d" % role[who], len(off))

    def evac(q, who, o):
        i = role[who] * O + o
        p = PLAN["tensor"].index(who) * O + o
        q.wait_ge(T.sem["s_mm%d" % i], 1)
        src, to = T["ps%d" % (p % BANKS)][:, 0:T_COLS], T.yb[:, i * T_COLS:(i + 1) * T_COLS]
        if q is g.scalar:
            c = q.activation(to, src, ActivationFunctionType.Copy)
        else:
            c = q.tensor_copy(to, src)
        c.then_inc(T.sem["s_ev%d" % i], 1)

    for op in PLAN["scalar"]:
        op = op.split()
        if op[0] == "e":
            evac(g.scalar, op[1], int(op[2]))
            continue
        i, off16 = made[op[1]], T["li%d" % role[op[1]]]
        once("scalar", g.scalar, "s_b1", 16)
        list_wait("scalar", g.scalar, op[1])
        for t in range(4):
            k = (4 + t) * n
            g.scalar.activation(T["g%d" % i][:, t:4 * P:4], T.bk1[:, 0:4 * K].indirect(off16[:, k:k + n]),
                                ActivationFunctionType.Copy).then_inc(T.sem["s_g%d%d" % (i, t)], 1)

    for op in PLAN["vector"]:
        op = op.split()
        if op[0] == "e":
            evac(g.vector, op[1], int(op[2]))
        elif op[0] == "x":
            g.vector.wait_ge(T.sem.s_x, 16)
            g.vector.quantize_mx(T.xq[:, 0:T_COLS], T.xz[:, 0:T_COLS], T.xb[:, 0:4 * T_COLS]).then_inc(T.sem.s_xq, 1)
        else:
            i, s = made[op[1]], role[op[1]]
            once("vector", g.vector, "s_b0", 16)
            list_wait("vector", g.vector, op[1])
            for t in range(4):
                k = t * n
                g.vector.wait_ge(T.sem["s_g%d%d" % (i, t)], 1)
                g.vector.tensor_tensor(T["h%d" % i][:, t:4 * P:4], T.bk0[:, 0:4 * K].indirect(T["li%d" % s][:, k:k + n]),
                                       T["g%d" % i][:, t:4 * P:4], AluOpType.add).then_inc(T.sem["s_h%d" % i], 1)
            g.vector.wait_ge(T.sem["s_h%d" % i], 4)
            g.vector.quantize_mx(T["w%d" % s][:, 0:P], T["z%d" % s][:, 0:P],
                                 T["h%d" % i][:, 0:4 * P]).then_inc(T.sem["s_q%d" % i], 1)

    order = [(w, o) for w in PLAN["tensor"] for o in range(O)]
    g.tensor.wait_ge(T.sem.s_xq, 1)
    for p, (who, o) in enumerate(order):
        s = role[who]
        if o == 0:
            if who in made:
                g.tensor.wait_ge(T.sem["s_q%d" % made[who]], 1)
            else:
                g.tensor.wait_ge(T.sem["s_ar%d" % s], 2 * arrive[who])
        if p >= BANKS:
            pw, po = order[p - BANKS]
            g.tensor.wait_ge(T.sem["s_ev%d" % (role[pw] * O + po)], 1)
        g.tensor.matmul_mx(T["ps%d" % (p % BANKS)][:, 0:T_COLS], T["w%d" % s][:, o * W:(o + 1) * W],
                           T["z%d" % s][:, o * W:(o + 1) * W], T.xq[:, 0:T_COLS], T.xz[:, 0:T_COLS],
                           True, True).then_inc(T.sem["s_mm%d" % (s * O + o)], 1)

    for group in PLAN["store"]:
        ss = sorted(role[w] for w in group)
        for s in ss:
            for o in range(O):
                g.sync.wait_ge(T.sem["s_ev%d" % (s * O + o)], 1)
        a, b = ss[0] * O * T_COLS, (ss[-1] + 1) * O * T_COLS
        g.sync.dma_start(T.y[:, a:b], T.yb[:, a:b]).then_inc(T.sem.s_out, 16)
    g.sync.wait_ge(T.sem.s_out, 16 * len(PLAN["store"]))
